import numpy as np
import ml_dtypes


def mxq(x, axis, fmt="e4m3"):
    dtype, down = {"e4m3": (ml_dtypes.float8_e4m3fn, 7), "e5m2": (ml_dtypes.float8_e5m2, 14)}[fmt]
    v = np.moveaxis(np.asarray(x, np.float32).astype(ml_dtypes.bfloat16).astype(np.float64), axis, -1)
    blocks = v.reshape(v.shape[:-1] + (-1, 32))
    amax = np.abs(blocks).max(-1, keepdims=True)
    byte = np.maximum(np.where(amax > 0, np.frexp(amax)[1] - 1 + 127, 0) - down, 1)
    scale = np.exp2(byte - 127.0)
    codes = (blocks / scale).astype(np.float32).astype(dtype).astype(np.float64)
    return np.moveaxis((codes * scale).reshape(v.shape), -1, axis)


WIDE = False


def mx_kscale(k):
    if not WIDE:
        return np.ones(k)
    levels = np.array([10, -10, 5, -5, 0])
    if k % 512:
        return np.exp2(np.random.permutation(np.resize(levels, k // 32))).repeat(32)
    a = np.empty((k // 512, 16))
    for p in range(k // 512):
        a[p, :8] = np.random.permutation(np.resize(levels, 8))
        for g in range(8):
            far = levels[np.abs(levels - a[p, g]) >= 10]
            a[p, g + 8] = far[np.random.randint(len(far))]
    return np.exp2(a.ravel()).repeat(32)


def f64(x):
    return np.asarray(x).astype(np.float64)


def striped(idx):
    return np.tile(idx.reshape(-1, 16).T, (8, 1)).astype(np.uint16)


def unstriped(offs):
    return offs[:16].T.reshape(-1).astype(np.int64)


def pack_weight(w):
    k, n = w.shape
    w = f64(np.asarray(w, np.float32).astype(ml_dtypes.bfloat16)).reshape(k // 32, 32, n)
    amax = np.abs(w).max(1)
    byte = np.clip(np.where(amax > 0, np.frexp(amax)[1] - 1 + 127 - 7, 1), 1, 254)
    scaled = (w * np.exp2(127.0 - byte)[:, None, :]).reshape(k, n).astype(np.float32)
    words = np.ascontiguousarray(scaled.reshape(k // 512, 128, 4, n).transpose(0, 1, 3, 2)).astype(ml_dtypes.float8_e4m3fn).view(np.uint8)
    return words, np.ascontiguousarray(byte.astype(np.uint8).reshape(k // 512, 16, n))


def unpack_weight(words, scales):
    g, p, n, _ = words.shape
    vals = np.ascontiguousarray(words).view(ml_dtypes.float8_e4m3fn).astype(np.float64) * np.repeat(np.exp2(scales.astype(np.float64) - 127.0), 8, axis=1)[..., None]
    return vals.transpose(0, 1, 3, 2).reshape(g * 512, n)


K, T, S, N, H, U = 512, 2048, 512, 128, 512, 1024


def setup_inputs():
    n = np.random.standard_normal
    s = mx_kscale(K)[:, None]
    u = mx_kscale(H)
    packed_xT = pack_weight(n((K, T)) * s)
    return {
        "x_words": packed_xT[0],
        "x_scales": packed_xT[1],
        "w1": (n((K, H)) / np.sqrt(K) / s).astype(np.float32),
        "w2": (n((K, H)) / np.sqrt(K) / s).astype(np.float32),
        "ask": (n((H, U))).astype(np.float32),
        "unit": (np.random.uniform(0.6, 1.4, (H, 1)) * u[:, None]).astype(np.float32),
        "w3": (n((H, N)) / np.sqrt(H) / u[:, None]).astype(np.float32),
        "offs": striped(np.random.permutation(T)[:S]),
        "use": striped(np.random.permutation(np.concatenate([np.arange(S), np.random.randint(0, S, U - S)]))),
        "alt1": striped(np.random.permutation(np.concatenate([np.arange(S), np.random.randint(0, S, U - S)]))),
        "alt2": striped(np.random.permutation(np.concatenate([np.arange(S), np.random.randint(0, S, U - S)]))),
    }


def reference(x_words, x_scales, w1, w2, ask, unit, w3, offs, use, alt1, alt2):
    xq = unpack_weight(x_words, x_scales)[:, unstriped(offs)]
    y = mxq(f64(w1), 0, "e4m3").T @ xq
    yu = y[:, unstriped(use)]
    z1 = mxq(f64(w2), 0, "e4m3").T @ xq
    z_1 = z1[:, unstriped(alt1)]
    z_2 = z1[:, unstriped(alt2)]
    hid = f64(unit) * (yu * f64(ask) - np.maximum(z_1, z_2))
    return mxq(f64(w3), 0, "e4m3").T @ mxq(hid, 0, "e4m3")

@@ -1,0 +1,180 @@
+from contextlib import ExitStack
+
+import concourse.mybir as mybir
+
+F32 = mybir.dt.float32
+BF16 = mybir.dt.bfloat16
+I32 = mybir.dt.int32
+U32 = mybir.dt.uint32
+U16 = mybir.dt.uint16
+U8 = mybir.dt.uint8
+FP8X4 = mybir.dt.float8_e4m3fn_x4
+ALU = mybir.AluOpType
+COPY = mybir.ActivationFunctionType.Copy
+
+K, T, S, N, H, U = 512, 2048, 512, 128, 512, 1024
+FLOPS = 2 * K * H * S * 2 + 2 * H * N * U
+
+P = 128
+PACK = 4
+SPARE = 32
+CHUNKS = ((0, 512), (512, 256), (768, 256))
+
+
+def tile_picked_ytoolrt_marg_p_kernel(
+    tc, x_words, x_scales, w1, w2, ask, unit, w3, offs, use, alt1, alt2, out
+):
+    nc = tc.nc
+    with ExitStack() as ctx:
+        keep = ctx.enter_context(tc.tile_pool(name="keep", bufs=1))
+        psum = ctx.enter_context(tc.psum_pool(name="psum", bufs=8))
+
+        def load_list(dram, name):
+            tile = keep.tile(list(dram.shape), U16, name=name)
+            nc.sync.dma_start(tile[:], dram)
+            return tile
+
+        def load_rows(dram, width, name):
+            tile = keep.tile([P, PACK, width], F32, name=name)
+            nc.sync.dma_start(tile[:], dram.rearrange("(p j) c -> p j c", j=PACK))
+            return tile
+
+        scale_table = keep.tile([P, T], U8, name="scale_table")
+        nc.gpsimd.memset(scale_table[:].bitcast(I32), 0)
+        w2_raw = load_rows(w2, H, "w2_raw")
+        offs_sb = load_list(offs, "offs_sb")
+        for r in range(4):
+            nc.sync.dma_start(scale_table[r:P:32, :].bitcast(I32), x_scales[0, r:16:4, :].bitcast(I32))
+        word_table = keep.tile([P, T], I32, name="word_table")
+        nc.sync.dma_start(word_table[:], x_words[0].rearrange("p n t -> p (n t)").bitcast(I32))
+        alt1_sb = load_list(alt1, "alt1_sb")
+        unit_sb = keep.tile([P, PACK], F32, name="unit_sb")
+        nc.sync.dma_start(unit_sb[:], unit.rearrange("(p t) o -> p (t o)", t=PACK))
+        alt2_sb = load_list(alt2, "alt2_sb")
+        w1_raw = load_rows(w1, H, "w1_raw")
+        use_sb = load_list(use, "use_sb")
+        ask_sb = [load_rows(ask[:, CHUNKS[0][0] : CHUNKS[0][0] + CHUNKS[0][1]], CHUNKS[0][1], "ask0")]
+        w3_raw = load_rows(w3, N, "w3_raw")
+        for c, (r0, n) in enumerate(CHUNKS[1:]):
+            ask_sb.append(load_rows(ask[:, r0 : r0 + n], n, "ask%d" % (c + 1)))
+
+        y_win = [keep.tile([P, S + SPARE], F32, name="y_win%d" % t) for t in range(PACK)]
+        z_win = [keep.tile([P, S + SPARE], F32, name="z_win%d" % t) for t in range(PACK)]
+        for win in z_win + y_win:
+            nc.vector.memset(win[:, S:], 0.0)
+
+        x_scale = keep.tile([P, S], U8, name="x_scale", align_bytes=64)
+        nc.vector.tensor_copy(x_scale[:], scale_table[:].indirect(offs_sb[:]))
+
+        def quantise_projection(raw, name, movers):
+            halves = []
+            rounded = []
+            for u in range(2):
+                pair = keep.tile([P, 2, P, PACK], BF16, name="%s_bf%d" % (name, u), align_bytes=64)
+                movers[u](
+                    pair[:].rearrange("p i m j -> p m j i"),
+                    raw[:].rearrange("p j (m u i) -> p u m j i", u=2, i=2)[:, u],
+                )
+                rounded.append(pair)
+            for u in range(2):
+                codes = keep.tile([P, 2 * P], U32, name="%s_codes%d" % (name, u), align_bytes=64)
+                scales = keep.tile([P, 2 * P], U8, name="%s_scales%d" % (name, u), align_bytes=64)
+                nc.vector.quantize_mx(
+                    out=codes[:].bitcast(FP8X4),
+                    scales=scales[:],
+                    in_=rounded[u][:].rearrange("p i m j -> p (i m j)"),
+                )
+                halves.append((codes, scales))
+            return halves
+
+        w2_q = quantise_projection(w2_raw, "w2", (nc.vector.tensor_copy, nc.scalar.copy))
+        x_codes = keep.tile([P, S], U32, name="x_codes", align_bytes=64)
+        nc.vector.tensor_copy(x_codes[:], word_table[:].bitcast(U32).indirect(offs_sb[:]))
+
+        sign = keep.tile([P, PACK], F32, name="sign")
+        size = keep.tile([P, PACK], F32, name="size")
+        minus_size = keep.tile([P, PACK], F32, name="minus_size")
+        step = keep.tile([P, PACK], F32, name="step")
+        nc.gpsimd.tensor_scalar(step[:], unit_sb[:], 0.0, 2.0, ALU.is_ge, ALU.mult)
+        nc.gpsimd.tensor_scalar(sign[:], step[:], 1.0, -1.0, ALU.mult, ALU.add)
+        nc.gpsimd.tensor_tensor(size[:], unit_sb[:], sign[:], ALU.mult)
+        nc.gpsimd.tensor_scalar(minus_size[:], size[:], -1.0, 0.0, ALU.mult, ALU.add)
+
+        def project(halves, t):
+            codes, scales = halves[t // 2]
+            cols = slice((t % 2) * P, (t % 2 + 1) * P)
+            acc = psum.tile([P, S], F32, name="acc")
+            nc.tensor.matmul_mx(
+                out=acc[:],
+                lhsT=codes[:, cols].bitcast(FP8X4),
+                lhsT_scale=scales[:, cols],
+                rhs=x_codes[:].bitcast(FP8X4),
+                rhs_scale=x_scale[:],
+                start=True,
+                stop=True,
+            )
+            return acc
+
+        z_acc = [project(w2_q, t) for t in range(PACK)]
+        w1_q = quantise_projection(w1_raw, "w1", (nc.vector.tensor_copy, nc.vector.tensor_copy))
+        y_acc = [project(w1_q, t) for t in range(PACK)]
+
+        w3_codes = keep.tile([P, N], U32, name="w3_codes", align_bytes=64)
+        w3_scales = keep.tile([P, N], U8, name="w3_scales", align_bytes=64)
+
+        def quantise_w3():
+            w3_bf = keep.tile([P, N, PACK], BF16, name="w3_bf", align_bytes=64)
+            nc.vector.tensor_tensor(
+                w3_bf[:].rearrange("p (c i) j -> p c j i", i=2),
+                w3_raw[:].rearrange("p j (c i) -> p c j i", i=2),
+                sign[:].rearrange("p (a j b) -> p a j b", a=1, b=1).to_broadcast([P, N // 2, PACK, 2]),
+                ALU.mult,
+            )
+            nc.vector.quantize_mx(
+                out=w3_codes[:].bitcast(FP8X4), scales=w3_scales[:], in_=w3_bf[:].rearrange("p n j -> p (n j)")
+            )
+
+        for c, (r0, n) in enumerate(CHUNKS):
+            cols = slice(r0 // 16, (r0 + n) // 16)
+            first = keep.tile([P, PACK, n], F32, name="first%d" % c)
+            second = keep.tile([P, PACK, n], F32, name="second%d" % c)
+            least = keep.tile([P, PACK, n], F32, name="least%d" % c)
+            used = keep.tile([P, PACK, n], F32, name="used%d" % c)
+            for t in range(PACK):
+                if c == 0:
+                    nc.scalar.activation(z_win[t][:, :S], z_acc[t][:], COPY, scale=minus_size[:, t : t + 1])
+                    nc.vector.tensor_scalar(y_win[t][:, :S], y_acc[t][:], size[:, t : t + 1], None, ALU.mult)
+                nc.scalar.activation(first[:, t, :], z_win[t][:].indirect(alt1_sb[:, cols]), COPY)
+                nc.scalar.activation(second[:, t, :], z_win[t][:].indirect(alt2_sb[:, cols]), COPY)
+                nc.vector.tensor_tensor(used[:, t, :], y_win[t][:].indirect(use_sb[:, cols]), ask_sb[c][:, t, :], ALU.mult)
+                if t % 2 == 1:
+                    nc.vector.tensor_tensor(
+                        least[:, t - 1 : t + 1, :], first[:, t - 1 : t + 1, :], second[:, t - 1 : t + 1, :], ALU.min
+                    )
+            if c == 0:
+                quantise_w3()
+            hid_bf = keep.tile([P, n, PACK], BF16, name="hid_bf%d" % c, align_bytes=64)
+            nc.vector.tensor_tensor(
+                hid_bf[:].rearrange("p (c i) t -> p c t i", i=2),
+                used[:].rearrange("p t (c i) -> p c t i", i=2),
+                least[:].rearrange("p t (c i) -> p c t i", i=2),
+                ALU.add,
+            )
+            hid_codes = keep.tile([P, n], U32, name="hid_codes%d" % c, align_bytes=64)
+            hid_scales = keep.tile([P, n], U8, name="hid_scales%d" % c, align_bytes=64)
+            nc.vector.quantize_mx(
+                out=hid_codes[:].bitcast(FP8X4), scales=hid_scales[:], in_=hid_bf[:].rearrange("p n t -> p (n t)")
+            )
+            acc = psum.tile([P, n], F32, name="acc")
+            nc.tensor.matmul_mx(
+                out=acc[:],
+                lhsT=w3_codes[:].bitcast(FP8X4),
+                lhsT_scale=w3_scales[:],
+                rhs=hid_codes[:].bitcast(FP8X4),
+                rhs_scale=hid_scales[:],
+                start=True,
+                stop=True,
+            )
+            result = keep.tile([P, n], F32, name="result%d" % c)
+            nc.scalar.copy(result[:], acc[:])
+            nc.sync.dma_start(out[:, r0 : r0 + n], result[:])

@@ -18,7 +18,9 @@ FLOPS = 2 * K * H * S * 2 + 2 * H * N * U
 P = 128
 PACK = 4
 SPARE = 32
-CHUNKS = ((0, 512), (512, 256), (768, 256))
+HALF = U // 2
+LAST = 128
+MOST = HALF - LAST
 
 
 def tile_picked_ytoolrt_marg_p_kernel(
@@ -34,29 +36,28 @@ def tile_picked_ytoolrt_marg_p_kernel(
             nc.sync.dma_start(tile[:], dram)
             return tile
 
-        def load_rows(dram, width, name):
-            tile = keep.tile([P, PACK, width], F32, name=name)
+        def load_rows(dram, width, name, tag=""):
+            tile = keep.tile([P, PACK, width], F32, name=name, tag=tag)
             nc.sync.dma_start(tile[:], dram.rearrange("(p j) c -> p j c", j=PACK))
             return tile
 
         scale_table = keep.tile([P, T], U8, name="scale_table")
         nc.gpsimd.memset(scale_table[:].bitcast(I32), 0)
-        w2_raw = load_rows(w2, H, "w2_raw")
+        unit_sb = keep.tile([P, PACK], F32, name="unit_sb")
+        nc.gpsimd.dma_start(unit_sb[:], unit.rearrange("(p t) o -> p (t o)", t=PACK))
         offs_sb = load_list(offs, "offs_sb")
-        for r in range(4):
-            nc.sync.dma_start(scale_table[r:P:32, :].bitcast(I32), x_scales[0, r:16:4, :].bitcast(I32))
+        alt1_sb = load_list(alt1, "alt1_sb")
         word_table = keep.tile([P, T], I32, name="word_table")
         nc.sync.dma_start(word_table[:], x_words[0].rearrange("p n t -> p (n t)").bitcast(I32))
-        alt1_sb = load_list(alt1, "alt1_sb")
-        unit_sb = keep.tile([P, PACK], F32, name="unit_sb")
-        nc.sync.dma_start(unit_sb[:], unit.rearrange("(p t) o -> p (t o)", t=PACK))
+        for r in range(4):
+            nc.sync.dma_start(scale_table[r:P:32, :].bitcast(I32), x_scales[0, r:16:4, :].bitcast(I32))
+        w2_raw = [load_rows(w2[:, h * H // 2 : (h + 1) * H // 2], H // 2, "w2_raw%d" % h) for h in range(2)]
+        w1_raw = [load_rows(w1, H, "w1_raw", "w1_then_second")]
         alt2_sb = load_list(alt2, "alt2_sb")
-        w1_raw = load_rows(w1, H, "w1_raw")
         use_sb = load_list(use, "use_sb")
-        ask_sb = [load_rows(ask[:, CHUNKS[0][0] : CHUNKS[0][0] + CHUNKS[0][1]], CHUNKS[0][1], "ask0")]
+        ask_sb = [load_rows(ask[:, :HALF], HALF, "ask0")]
         w3_raw = load_rows(w3, N, "w3_raw")
-        for c, (r0, n) in enumerate(CHUNKS[1:]):
-            ask_sb.append(load_rows(ask[:, r0 : r0 + n], n, "ask%d" % (c + 1)))
+        ask_sb.append(load_rows(ask[:, HALF:], HALF, "ask1"))
 
         y_win = [keep.tile([P, S + SPARE], F32, name="y_win%d" % t) for t in range(PACK)]
         z_win = [keep.tile([P, S + SPARE], F32, name="z_win%d" % t) for t in range(PACK)]
@@ -66,30 +67,30 @@ def tile_picked_ytoolrt_marg_p_kernel(
         x_scale = keep.tile([P, S], U8, name="x_scale", align_bytes=64)
         nc.vector.tensor_copy(x_scale[:], scale_table[:].indirect(offs_sb[:]))
 
-        def quantise_projection(raw, name, movers):
-            halves = []
-            rounded = []
-            for u in range(2):
-                pair = keep.tile([P, 2, P, PACK], BF16, name="%s_bf%d" % (name, u), align_bytes=64)
-                movers[u](
-                    pair[:].rearrange("p i m j -> p m j i"),
-                    raw[:].rearrange("p j (m u i) -> p u m j i", u=2, i=2)[:, u],
-                )
-                rounded.append(pair)
-            for u in range(2):
-                codes = keep.tile([P, 2 * P], U32, name="%s_codes%d" % (name, u), align_bytes=64)
-                scales = keep.tile([P, 2 * P], U8, name="%s_scales%d" % (name, u), align_bytes=64)
-                nc.vector.quantize_mx(
-                    out=codes[:].bitcast(FP8X4),
-                    scales=scales[:],
-                    in_=rounded[u][:].rearrange("p i m j -> p (i m j)"),
-                )
-                halves.append((codes, scales))
-            return halves
-
-        w2_q = quantise_projection(w2_raw, "w2", (nc.vector.tensor_copy, nc.scalar.copy))
         x_codes = keep.tile([P, S], U32, name="x_codes", align_bytes=64)
         nc.vector.tensor_copy(x_codes[:], word_table[:].bitcast(U32).indirect(offs_sb[:]))
+
+        def round_pair(pieces, u, mover, name):
+            pair = keep.tile([P, 2, P, PACK], BF16, name=name, align_bytes=64)
+            span = P // len(pieces)
+            for h, raw in enumerate(pieces):
+                mover(
+                    pair[:, :, h * span : (h + 1) * span, :].rearrange("p i m j -> p m j i"),
+                    raw[:].rearrange("p j (m u i) -> p u m j i", u=2, i=2)[:, u],
+                )
+            return pair
+
+        def quantise(rounded, n, name):
+            codes = keep.tile([P, n], U32, name=name + "_codes", align_bytes=64)
+            scales = keep.tile([P, n], U8, name=name + "_scales", align_bytes=64)
+            nc.vector.quantize_mx(out=codes[:].bitcast(FP8X4), scales=scales[:], in_=rounded)
+            return codes, scales
+
+        def quantise_pair(pair, name):
+            return quantise(pair[:].rearrange("p i m j -> p (i m j)"), 2 * P, name)
+
+        w2_bf = [round_pair(w2_raw, 0, nc.vector.tensor_copy, "w2_bf0"), round_pair(w2_raw, 1, nc.scalar.copy, "w2_bf1")]
+        w2_q = [quantise_pair(w2_bf[u], "w2_%d" % u) for u in range(2)]
 
         sign = keep.tile([P, PACK], F32, name="sign")
         size = keep.tile([P, PACK], F32, name="size")
@@ -100,81 +101,138 @@ def tile_picked_ytoolrt_marg_p_kernel(
         nc.gpsimd.tensor_tensor(size[:], unit_sb[:], sign[:], ALU.mult)
         nc.gpsimd.tensor_scalar(minus_size[:], size[:], -1.0, 0.0, ALU.mult, ALU.add)
 
-        def project(halves, t):
+        def project(halves, t, j0=0, n=S):
             codes, scales = halves[t // 2]
             cols = slice((t % 2) * P, (t % 2 + 1) * P)
-            acc = psum.tile([P, S], F32, name="acc")
+            acc = psum.tile([P, n], F32, name="acc")
             nc.tensor.matmul_mx(
                 out=acc[:],
                 lhsT=codes[:, cols].bitcast(FP8X4),
                 lhsT_scale=scales[:, cols],
-                rhs=x_codes[:].bitcast(FP8X4),
-                rhs_scale=x_scale[:],
+                rhs=x_codes[:, j0 : j0 + n].bitcast(FP8X4),
+                rhs_scale=x_scale[:, j0 : j0 + n],
                 start=True,
                 stop=True,
             )
             return acc
 
-        z_acc = [project(w2_q, t) for t in range(PACK)]
-        w1_q = quantise_projection(w1_raw, "w1", (nc.vector.tensor_copy, nc.vector.tensor_copy))
-        y_acc = [project(w1_q, t) for t in range(PACK)]
+        first = [keep.tile([P, PACK, HALF], F32, name="first%d" % h) for h in range(2)]
+        used = [keep.tile([P, PACK, HALF], F32, name="used%d" % h) for h in range(2)]
 
-        w3_codes = keep.tile([P, N], U32, name="w3_codes", align_bytes=64)
-        w3_scales = keep.tile([P, N], U8, name="w3_scales", align_bytes=64)
+        def empty_on_scalar(win, acc, factor):
+            nc.scalar.activation(win, acc[:], COPY, scale=factor)
 
-        def quantise_w3():
-            w3_bf = keep.tile([P, N, PACK], BF16, name="w3_bf", align_bytes=64)
-            nc.vector.tensor_tensor(
-                w3_bf[:].rearrange("p (c i) j -> p c j i", i=2),
-                w3_raw[:].rearrange("p j (c i) -> p c j i", i=2),
-                sign[:].rearrange("p (a j b) -> p a j b", a=1, b=1).to_broadcast([P, N // 2, PACK, 2]),
-                ALU.mult,
-            )
-            nc.vector.quantize_mx(
-                out=w3_codes[:].bitcast(FP8X4), scales=w3_scales[:], in_=w3_bf[:].rearrange("p n j -> p (n j)")
-            )
+        def empty_on_vector(win, acc, factor):
+            nc.vector.tensor_scalar(win, acc[:], factor, None, ALU.mult)
 
-        for c, (r0, n) in enumerate(CHUNKS):
-            cols = slice(r0 // 16, (r0 + n) // 16)
-            first = keep.tile([P, PACK, n], F32, name="first%d" % c)
-            second = keep.tile([P, PACK, n], F32, name="second%d" % c)
-            least = keep.tile([P, PACK, n], F32, name="least%d" % c)
-            used = keep.tile([P, PACK, n], F32, name="used%d" % c)
-            for t in range(PACK):
-                if c == 0:
-                    nc.scalar.activation(z_win[t][:, :S], z_acc[t][:], COPY, scale=minus_size[:, t : t + 1])
-                    nc.vector.tensor_scalar(y_win[t][:, :S], y_acc[t][:], size[:, t : t + 1], None, ALU.mult)
-                nc.scalar.activation(first[:, t, :], z_win[t][:].indirect(alt1_sb[:, cols]), COPY)
-                nc.scalar.activation(second[:, t, :], z_win[t][:].indirect(alt2_sb[:, cols]), COPY)
-                nc.vector.tensor_tensor(used[:, t, :], y_win[t][:].indirect(use_sb[:, cols]), ask_sb[c][:, t, :], ALU.mult)
-                if t % 2 == 1:
-                    nc.vector.tensor_tensor(
-                        least[:, t - 1 : t + 1, :], first[:, t - 1 : t + 1, :], second[:, t - 1 : t + 1, :], ALU.min
-                    )
-            if c == 0:
-                quantise_w3()
-            hid_bf = keep.tile([P, n, PACK], BF16, name="hid_bf%d" % c, align_bytes=64)
+        def fetch_other(into, offsets, h, t, r0, n):
+            cols = slice((h * HALF + r0) // 16, (h * HALF + r0 + n) // 16)
+            nc.scalar.activation(into[h][:, t, r0 : r0 + n], z_win[t][:].indirect(offsets[:, cols]), COPY)
+
+        def fetch_others(h, t, r0, n):
+            fetch_other(first, alt1_sb, h, t, r0, n)
+            fetch_other(second, alt2_sb, h, t, r0, n)
+
+        def fetch_used(h, t):
+            cols = slice(h * HALF // 16, (h + 1) * HALF // 16)
+            nc.vector.tensor_tensor(used[h][:, t, :], y_win[t][:].indirect(use_sb[:, cols]), ask_sb[h][:, t, :], ALU.mult)
+
+        def lesser(least, h, planes, r0):
+            cols = slice(r0, r0 + least.shape[2])
+            nc.vector.tensor_tensor(least[:, planes, :], first[h][:, planes, cols], second[h][:, planes, cols], ALU.min)
+
+        def join(least, h, r0):
+            n = least.shape[2]
+            hid_bf = keep.tile([P, n, PACK], BF16, name="hid_bf%d_%d" % (h, r0), align_bytes=64)
             nc.vector.tensor_tensor(
                 hid_bf[:].rearrange("p (c i) t -> p c t i", i=2),
-                used[:].rearrange("p t (c i) -> p c t i", i=2),
+                used[h][:, :, r0 : r0 + n].rearrange("p t (c i) -> p c t i", i=2),
                 least[:].rearrange("p t (c i) -> p c t i", i=2),
                 ALU.add,
             )
-            hid_codes = keep.tile([P, n], U32, name="hid_codes%d" % c, align_bytes=64)
-            hid_scales = keep.tile([P, n], U8, name="hid_scales%d" % c, align_bytes=64)
-            nc.vector.quantize_mx(
-                out=hid_codes[:].bitcast(FP8X4), scales=hid_scales[:], in_=hid_bf[:].rearrange("p n t -> p (n t)")
-            )
+            return hid_bf
+
+        def finish(hid_bf, r0, widths):
+            n = sum(widths)
+            hid_codes, hid_scales = quantise(hid_bf[:].rearrange("p n t -> p (n t)"), n, "hid%d" % r0)
             acc = psum.tile([P, n], F32, name="acc")
-            nc.tensor.matmul_mx(
-                out=acc[:],
-                lhsT=w3_codes[:].bitcast(FP8X4),
-                lhsT_scale=w3_scales[:],
-                rhs=hid_codes[:].bitcast(FP8X4),
-                rhs_scale=hid_scales[:],
-                start=True,
-                stop=True,
-            )
-            result = keep.tile([P, n], F32, name="result%d" % c)
+            at = 0
+            for width in widths:
+                cols = slice(at, at + width)
+                nc.tensor.matmul_mx(
+                    out=acc[:, cols],
+                    lhsT=w3_codes[:].bitcast(FP8X4),
+                    lhsT_scale=w3_scales[:],
+                    rhs=hid_codes[:, cols].bitcast(FP8X4),
+                    rhs_scale=hid_scales[:, cols],
+                    start=True,
+                    stop=True,
+                )
+                at = at + width
+            result = keep.tile([P, n], F32, name="result%d" % r0)
             nc.scalar.copy(result[:], acc[:])
             nc.sync.dma_start(out[:, r0 : r0 + n], result[:])
+
+        z0_left = project(w2_q, 0, 0, S // 2)
+        z0_right = project(w2_q, 0, S // 2, S // 2)
+        z_acc = [None] + [project(w2_q, t) for t in range(1, PACK)]
+        empty_on_scalar(z_win[0][:, : S // 2], z0_left, minus_size[:, 0:1])
+        empty_on_vector(z_win[0][:, S // 2 : S], z0_right, minus_size[:, 0:1])
+        empty_on_vector(z_win[1][:, :S], z_acc[1], minus_size[:, 1:2])
+        fetch_other(first, alt1_sb, 0, 0, 0, HALF)
+        w1_bf = [round_pair(w1_raw, 0, nc.vector.tensor_copy, "w1_bf0"), round_pair(w1_raw, 1, nc.scalar.copy, "w1_bf1")]
+        second = [
+            keep.tile([P, PACK, HALF], F32, name="second0", tag="w1_then_second"),
+            keep.tile([P, PACK, HALF], F32, name="second1"),
+        ]
+        fetch_other(second, alt2_sb, 0, 0, 0, HALF)
+        w1_q = [quantise_pair(w1_bf[0], "w1_0")]
+        y_acc = [project(w1_q, t) for t in range(2)]
+        for t in range(2):
+            empty_on_vector(y_win[t][:, :S], y_acc[t], size[:, t : t + 1])
+        fetch_used(0, 0)
+        w1_q.append(quantise_pair(w1_bf[1], "w1_1"))
+        y_acc.extend([project(w1_q, t) for t in range(2, PACK)])
+        fetch_used(0, 1)
+        for t in range(2, PACK):
+            empty_on_vector(y_win[t][:, :S], y_acc[t], size[:, t : t + 1])
+
+        fetch_others(0, 1, 0, HALF)
+        for t in range(2, PACK):
+            empty_on_scalar(z_win[t][:, :S], z_acc[t], minus_size[:, t : t + 1])
+            fetch_others(0, t, 0, HALF)
+        for t in range(PACK - 1):
+            fetch_others(1, t, 0, HALF)
+        fetch_others(1, PACK - 1, 0, MOST)
+        fetch_others(1, PACK - 1, MOST, LAST)
+
+        least0 = keep.tile([P, PACK, HALF], F32, name="least0")
+        least1 = keep.tile([P, PACK, MOST], F32, name="least1")
+        least2 = keep.tile([P, PACK, LAST], F32, name="least2")
+
+        w3_bf = keep.tile([P, N, PACK], BF16, name="w3_bf", align_bytes=64)
+        nc.vector.tensor_tensor(
+            w3_bf[:].rearrange("p (c i) j -> p c j i", i=2),
+            w3_raw[:].rearrange("p j (c i) -> p c j i", i=2),
+            sign[:].rearrange("p (a j b) -> p a j b", a=1, b=1).to_broadcast([P, N // 2, PACK, 2]),
+            ALU.mult,
+        )
+        fetch_used(0, 2)
+        w3_codes, w3_scales = quantise(w3_bf[:].rearrange("p n j -> p (n j)"), N, "w3")
+        lesser(least0, 0, slice(0, 2), 0)
+        fetch_used(0, 3)
+        fetch_used(1, 0)
+        fetch_used(1, 1)
+        lesser(least0, 0, slice(2, 4), 0)
+        fetch_used(1, 2)
+        hid0 = join(least0, 0, 0)
+        fetch_used(1, 3)
+        finish(hid0, 0, [HALF])
+        lesser(least1, 1, slice(0, 3), 0)
+        lesser(least2, 1, slice(0, 3), MOST)
+        lesser(least1, 1, slice(3, 4), 0)
+        hid1 = join(least1, 1, 0)
+        lesser(least2, 1, slice(3, 4), MOST)
+        finish(hid1, HALF, [256, 128])
+        hid2 = join(least2, 1, MOST)
+        finish(hid2, HALF + MOST, [LAST])

from contextlib import ExitStack

import concourse.mybir as mybir

F32 = mybir.dt.float32
BF16 = mybir.dt.bfloat16
I32 = mybir.dt.int32
U32 = mybir.dt.uint32
U16 = mybir.dt.uint16
U8 = mybir.dt.uint8
FP8X4 = mybir.dt.float8_e4m3fn_x4
ALU = mybir.AluOpType
COPY = mybir.ActivationFunctionType.Copy

K, T, S, N, H, U = 512, 2048, 512, 128, 512, 1024
FLOPS = 2 * K * H * S * 2 + 2 * H * N * U

P = 128
PACK = 4
SPARE = 32
HALF = U // 2
LAST = 128
MOST = HALF - LAST


def tile_picked_ytoolrt_marg_p_kernel(
    tc, x_words, x_scales, w1, w2, ask, unit, w3, offs, use, alt1, alt2, out
):
    nc = tc.nc
    with ExitStack() as ctx:
        keep = ctx.enter_context(tc.tile_pool(name="keep", bufs=1))
        psum = ctx.enter_context(tc.psum_pool(name="psum", bufs=8))

        def load_list(dram, name):
            tile = keep.tile(list(dram.shape), U16, name=name)
            nc.sync.dma_start(tile[:], dram)
            return tile

        def load_rows(dram, width, name, tag=""):
            tile = keep.tile([P, PACK, width], F32, name=name, tag=tag)
            nc.sync.dma_start(tile[:], dram.rearrange("(p j) c -> p j c", j=PACK))
            return tile

        scale_table = keep.tile([P, T], U8, name="scale_table")
        nc.gpsimd.memset(scale_table[:].bitcast(I32), 0)
        unit_sb = keep.tile([P, PACK], F32, name="unit_sb")
        nc.gpsimd.dma_start(unit_sb[:], unit.rearrange("(p t) o -> p (t o)", t=PACK))
        offs_sb = load_list(offs, "offs_sb")
        alt1_sb = load_list(alt1, "alt1_sb")
        word_table = keep.tile([P, T], I32, name="word_table")
        nc.sync.dma_start(word_table[:], x_words[0].rearrange("p n t -> p (n t)").bitcast(I32))
        for r in range(4):
            nc.sync.dma_start(scale_table[r:P:32, :].bitcast(I32), x_scales[0, r:16:4, :].bitcast(I32))
        w2_raw = [load_rows(w2[:, h * H // 2 : (h + 1) * H // 2], H // 2, "w2_raw%d" % h) for h in range(2)]
        w1_raw = [load_rows(w1, H, "w1_raw", "w1_then_second")]
        alt2_sb = load_list(alt2, "alt2_sb")
        use_sb = load_list(use, "use_sb")
        ask_sb = [load_rows(ask[:, :HALF], HALF, "ask0")]
        w3_raw = load_rows(w3, N, "w3_raw")
        ask_sb.append(load_rows(ask[:, HALF:], HALF, "ask1"))

        y_win = [keep.tile([P, S + SPARE], F32, name="y_win%d" % t) for t in range(PACK)]
        z_win = [keep.tile([P, S + SPARE], F32, name="z_win%d" % t) for t in range(PACK)]
        for win in z_win + y_win:
            nc.vector.memset(win[:, S:], 0.0)

        x_scale = keep.tile([P, S], U8, name="x_scale", align_bytes=64)
        nc.vector.tensor_copy(x_scale[:], scale_table[:].indirect(offs_sb[:]))

        x_codes = keep.tile([P, S], U32, name="x_codes", align_bytes=64)
        nc.vector.tensor_copy(x_codes[:], word_table[:].bitcast(U32).indirect(offs_sb[:]))

        def round_pair(pieces, u, mover, name):
            pair = keep.tile([P, 2, P, PACK], BF16, name=name, align_bytes=64)
            span = P // len(pieces)
            for h, raw in enumerate(pieces):
                mover(
                    pair[:, :, h * span : (h + 1) * span, :].rearrange("p i m j -> p m j i"),
                    raw[:].rearrange("p j (m u i) -> p u m j i", u=2, i=2)[:, u],
                )
            return pair

        def quantise(rounded, n, name):
            codes = keep.tile([P, n], U32, name=name + "_codes", align_bytes=64)
            scales = keep.tile([P, n], U8, name=name + "_scales", align_bytes=64)
            nc.vector.quantize_mx(out=codes[:].bitcast(FP8X4), scales=scales[:], in_=rounded)
            return codes, scales

        def quantise_pair(pair, name):
            return quantise(pair[:].rearrange("p i m j -> p (i m j)"), 2 * P, name)

        w2_bf = [round_pair(w2_raw, 0, nc.vector.tensor_copy, "w2_bf0"), round_pair(w2_raw, 1, nc.scalar.copy, "w2_bf1")]
        w2_q = [quantise_pair(w2_bf[u], "w2_%d" % u) for u in range(2)]

        sign = keep.tile([P, PACK], F32, name="sign")
        size = keep.tile([P, PACK], F32, name="size")
        minus_size = keep.tile([P, PACK], F32, name="minus_size")
        step = keep.tile([P, PACK], F32, name="step")
        nc.gpsimd.tensor_scalar(step[:], unit_sb[:], 0.0, 2.0, ALU.is_ge, ALU.mult)
        nc.gpsimd.tensor_scalar(sign[:], step[:], 1.0, -1.0, ALU.mult, ALU.add)
        nc.gpsimd.tensor_tensor(size[:], unit_sb[:], sign[:], ALU.mult)
        nc.gpsimd.tensor_scalar(minus_size[:], size[:], -1.0, 0.0, ALU.mult, ALU.add)

        def project(halves, t, j0=0, n=S):
            codes, scales = halves[t // 2]
            cols = slice((t % 2) * P, (t % 2 + 1) * P)
            acc = psum.tile([P, n], F32, name="acc")
            nc.tensor.matmul_mx(
                out=acc[:],
                lhsT=codes[:, cols].bitcast(FP8X4),
                lhsT_scale=scales[:, cols],
                rhs=x_codes[:, j0 : j0 + n].bitcast(FP8X4),
                rhs_scale=x_scale[:, j0 : j0 + n],
                start=True,
                stop=True,
            )
            return acc

        first = [keep.tile([P, PACK, HALF], F32, name="first%d" % h) for h in range(2)]
        used = [keep.tile([P, PACK, HALF], F32, name="used%d" % h) for h in range(2)]

        def empty_on_scalar(win, acc, factor):
            nc.scalar.activation(win, acc[:], COPY, scale=factor)

        def empty_on_vector(win, acc, factor):
            nc.vector.tensor_scalar(win, acc[:], factor, None, ALU.mult)

        def fetch_other(into, offsets, h, t, r0, n):
            cols = slice((h * HALF + r0) // 16, (h * HALF + r0 + n) // 16)
            nc.scalar.activation(into[h][:, t, r0 : r0 + n], z_win[t][:].indirect(offsets[:, cols]), COPY)

        def fetch_others(h, t, r0, n):
            fetch_other(first, alt1_sb, h, t, r0, n)
            fetch_other(second, alt2_sb, h, t, r0, n)

        def fetch_used(h, t):
            cols = slice(h * HALF // 16, (h + 1) * HALF // 16)
            nc.vector.tensor_tensor(used[h][:, t, :], y_win[t][:].indirect(use_sb[:, cols]), ask_sb[h][:, t, :], ALU.mult)

        def lesser(least, h, planes, r0):
            cols = slice(r0, r0 + least.shape[2])
            nc.vector.tensor_tensor(least[:, planes, :], first[h][:, planes, cols], second[h][:, planes, cols], ALU.min)

        def join(least, h, r0):
            n = least.shape[2]
            hid_bf = keep.tile([P, n, PACK], BF16, name="hid_bf%d_%d" % (h, r0), align_bytes=64)
            nc.vector.tensor_tensor(
                hid_bf[:].rearrange("p (c i) t -> p c t i", i=2),
                used[h][:, :, r0 : r0 + n].rearrange("p t (c i) -> p c t i", i=2),
                least[:].rearrange("p t (c i) -> p c t i", i=2),
                ALU.add,
            )
            return hid_bf

        def finish(hid_bf, r0, widths):
            n = sum(widths)
            hid_codes, hid_scales = quantise(hid_bf[:].rearrange("p n t -> p (n t)"), n, "hid%d" % r0)
            acc = psum.tile([P, n], F32, name="acc")
            at = 0
            for width in widths:
                cols = slice(at, at + width)
                nc.tensor.matmul_mx(
                    out=acc[:, cols],
                    lhsT=w3_codes[:].bitcast(FP8X4),
                    lhsT_scale=w3_scales[:],
                    rhs=hid_codes[:, cols].bitcast(FP8X4),
                    rhs_scale=hid_scales[:, cols],
                    start=True,
                    stop=True,
                )
                at = at + width
            result = keep.tile([P, n], F32, name="result%d" % r0)
            nc.scalar.copy(result[:], acc[:])
            nc.sync.dma_start(out[:, r0 : r0 + n], result[:])

        z0_left = project(w2_q, 0, 0, S // 2)
        z0_right = project(w2_q, 0, S // 2, S // 2)
        z_acc = [None] + [project(w2_q, t) for t in range(1, PACK)]
        empty_on_scalar(z_win[0][:, : S // 2], z0_left, minus_size[:, 0:1])
        empty_on_vector(z_win[0][:, S // 2 : S], z0_right, minus_size[:, 0:1])
        empty_on_vector(z_win[1][:, :S], z_acc[1], minus_size[:, 1:2])
        fetch_other(first, alt1_sb, 0, 0, 0, HALF)
        w1_bf = [round_pair(w1_raw, 0, nc.vector.tensor_copy, "w1_bf0"), round_pair(w1_raw, 1, nc.scalar.copy, "w1_bf1")]
        second = [
            keep.tile([P, PACK, HALF], F32, name="second0", tag="w1_then_second"),
            keep.tile([P, PACK, HALF], F32, name="second1"),
        ]
        fetch_other(second, alt2_sb, 0, 0, 0, HALF)
        w1_q = [quantise_pair(w1_bf[0], "w1_0")]
        y_acc = [project(w1_q, t) for t in range(2)]
        for t in range(2):
            empty_on_vector(y_win[t][:, :S], y_acc[t], size[:, t : t + 1])
        fetch_used(0, 0)
        w1_q.append(quantise_pair(w1_bf[1], "w1_1"))
        y_acc.extend([project(w1_q, t) for t in range(2, PACK)])
        fetch_used(0, 1)
        for t in range(2, PACK):
            empty_on_vector(y_win[t][:, :S], y_acc[t], size[:, t : t + 1])

        fetch_others(0, 1, 0, HALF)
        for t in range(2, PACK):
            empty_on_scalar(z_win[t][:, :S], z_acc[t], minus_size[:, t : t + 1])
            fetch_others(0, t, 0, HALF)
        for t in range(PACK - 1):
            fetch_others(1, t, 0, HALF)
        fetch_others(1, PACK - 1, 0, MOST)
        fetch_others(1, PACK - 1, MOST, LAST)

        least0 = keep.tile([P, PACK, HALF], F32, name="least0")
        least1 = keep.tile([P, PACK, MOST], F32, name="least1")
        least2 = keep.tile([P, PACK, LAST], F32, name="least2")

        w3_bf = keep.tile([P, N, PACK], BF16, name="w3_bf", align_bytes=64)
        nc.vector.tensor_tensor(
            w3_bf[:].rearrange("p (c i) j -> p c j i", i=2),
            w3_raw[:].rearrange("p j (c i) -> p c j i", i=2),
            sign[:].rearrange("p (a j b) -> p a j b", a=1, b=1).to_broadcast([P, N // 2, PACK, 2]),
            ALU.mult,
        )
        fetch_used(0, 2)
        w3_codes, w3_scales = quantise(w3_bf[:].rearrange("p n j -> p (n j)"), N, "w3")
        lesser(least0, 0, slice(0, 2), 0)
        fetch_used(0, 3)
        fetch_used(1, 0)
        fetch_used(1, 1)
        lesser(least0, 0, slice(2, 4), 0)
        fetch_used(1, 2)
        hid0 = join(least0, 0, 0)
        fetch_used(1, 3)
        finish(hid0, 0, [HALF])
        lesser(least1, 1, slice(0, 3), 0)
        lesser(least2, 1, slice(0, 3), MOST)
        lesser(least1, 1, slice(3, 4), 0)
        hid1 = join(least1, 1, 0)
        lesser(least2, 1, slice(3, 4), MOST)
        finish(hid1, HALF, [256, 128])
        hid2 = join(least2, 1, MOST)
        finish(hid2, HALF + MOST, [LAST])
